import numpy as np
import ml_dtypes


def mxq(x, axis, fmt="e4m3"):
    dtype, down = {"e4m3": (ml_dtypes.float8_e4m3fn, 7), "e5m2": (ml_dtypes.float8_e5m2, 14)}[fmt]
    v = np.moveaxis(np.asarray(x, np.float32).astype(ml_dtypes.bfloat16).astype(np.float64), axis, -1)
    blocks = v.reshape(v.shape[:-1] + (-1, 32))
    amax = np.abs(blocks).max(-1, keepdims=True)
    byte = np.maximum(np.where(amax > 0, np.frexp(amax)[1] - 1 + 127, 0) - down, 1)
    scale = np.exp2(byte - 127.0)
    codes = (blocks / scale).astype(np.float32).astype(dtype).astype(np.float64)
    return np.moveaxis((codes * scale).reshape(v.shape), -1, axis)


WIDE = False


def mx_kscale(k, group=512):
    if not WIDE:
        return np.ones(k)
    levels = np.array([10, -10, 5, -5, 0])
    if group != 512:
        return np.exp2(np.random.permutation(np.resize(levels, k // group))).repeat(group)
    if k % 512:
        return np.exp2(np.random.permutation(np.resize(levels, k // 32))).repeat(32)
    a = np.empty((k // 512, 16))
    for p in range(k // 512):
        a[p, :8] = np.random.permutation(np.resize(levels, 8))
        for g in range(8):
            far = levels[np.abs(levels - a[p, g]) >= 10]
            a[p, g + 8] = far[np.random.randint(len(far))]
    return np.exp2(a.ravel()).repeat(32)


def f64(x):
    return np.asarray(x).astype(np.float64)


E2M1 = np.array([0.0, 0.5, 1.0, 1.5, 2.0, 3.0, 4.0, 6.0, -0.0, -0.5, -1.0, -1.5, -2.0, -3.0, -4.0, -6.0])


def pack_group(w):
    k, n = w.shape
    w = f64(np.asarray(w, np.float32).astype(ml_dtypes.bfloat16)).reshape(k // 32, 32, n)
    amax = np.abs(w).max(1)
    mant, ex = np.frexp(amax / 6.0)
    byte = np.clip(np.where(amax > 0, np.where(mant > 0.5, ex, ex - 1) + 127, 1), 1, 254)
    scaled = (w * np.exp2(127.0 - byte)[:, None, :]).reshape(k, n).astype(np.float32)
    c = np.ascontiguousarray(scaled.reshape(k // 4, 4, n).transpose(0, 2, 1)).astype(ml_dtypes.float4_e2m1fn).view(np.uint8) & 0xF
    return np.ascontiguousarray((c[..., 0::2] | (c[..., 1::2] << 4)).reshape(k // 4, 2 * n)), byte.astype(np.uint8)


def unpack_group(words, scales):
    p, n = words.shape[0], scales.shape[1]
    words = np.ascontiguousarray(words).reshape(p, n, 2)
    nib = np.empty((p, n, 4), np.uint8)
    nib[..., 0::2] = words & 0xF
    nib[..., 1::2] = words >> 4
    return E2M1[nib].transpose(0, 2, 1).reshape(4 * p, n) * np.repeat(np.exp2(scales.astype(np.float64) - 127.0), 32, axis=0)


G, D, M, O, N = 2, 256, 256, 256, 512


def setup_inputs():
    n = np.random.standard_normal
    s_d = mx_kscale(D, 0)
    s_o = mx_kscale(O, 0)
    w1_ = [pack_group(w) for w in n((G, D, M)) / np.sqrt(D) / s_d[:, None]]
    w2_ = [pack_group(w) for w in n((G, D, M)) / np.sqrt(D) / s_d[:, None]]
    wo_ = [pack_group(w) for w in n((G, O, M)) / np.sqrt(O) / s_o[:, None]]
    return {
        "x": (n((G, D, N)) * s_d[:, None]).astype(np.float32),
        "w1_words": np.stack([w[0] for w in w1_]),
        "w1_scales": np.stack([w[1] for w in w1_]),
        "w2_words": np.stack([w[0] for w in w2_]),
        "w2_scales": np.stack([w[1] for w in w2_]),
        "sh": (np.random.uniform(0.1, 0.4, (G, M, 1))).astype(np.float32),
        "d0": (np.random.uniform(2.0, 6.0, (G, M, N))).astype(np.float32),
        "wo_words": np.stack([w[0] for w in wo_]),
        "wo_scales": np.stack([w[1] for w in wo_]),
        "dy": (n((G, O, N)) * s_o[:, None]).astype(np.float32),
        "old": (0.3 * n((G, M, N))).astype(np.float32),
    }


def reference(x, w1_words, w1_scales, w2_words, w2_scales, sh, d0, wo_words, wo_scales, dy, old):
    w1 = np.stack([unpack_group(w1_words[g], w1_scales[g]) for g in range(G)])
    xq = mxq(f64(x), 1, "e4m3")
    z1 = w1.transpose(0, 2, 1) @ xq
    w2 = np.stack([unpack_group(w2_words[g], w2_scales[g]) for g in range(G)])
    z2 = w2.transpose(0, 2, 1) @ xq
    q1 = f64(d0) - z1 * 2.0
    wo = np.stack([unpack_group(wo_words[g], wo_scales[g]) for g in range(G)])
    dyq = mxq(f64(dy), 1, "e4m3")
    c0 = wo.transpose(0, 2, 1) @ dyq
    dq1 = c0 * z2 * np.exp(q1 * f64(sh) * (-1.0)) * (-1.0) * f64(sh)
    dz1 = dq1 * (-1.0) * 2.0
    y = dz1 + f64(old)
    return y

@@ -1,0 +1,201 @@
+from contextlib import ExitStack
+
+import concourse.mybir as mybir
+
+G, D, M, N = 2, 256, 256, 512
+FLOPS = 3 * 2 * G * D * M * N
+
+F32 = mybir.dt.float32
+BF16 = mybir.dt.bfloat16
+I32 = mybir.dt.int32
+U32 = mybir.dt.uint32
+U8 = mybir.dt.uint8
+FP8X4 = mybir.dt.float8_e4m3fn_x4
+FP4X4 = mybir.dt.float4_e2m1fn_x4
+ALU = mybir.AluOpType
+ACT = mybir.ActivationFunctionType
+
+P = 128
+PACK = 4
+ROWS = D // PACK
+QUAD = 32
+HALF = N // 2
+TILES = [(g, h) for h in range(M // P) for g in range(G)]
+X_VECTOR_COLS = 352
+DY_VECTOR_COLS = 176
+
+
+def interleave(copy, packed, raw, c0, c1):
+    copy(
+        out=packed[:, c0:c1, :].rearrange("p (c i) j -> p c j i", i=4),
+        in_=raw[:, :, c0:c1].rearrange("p j (c i) -> p c j i", i=4),
+    )
+
+
+def tile_rows_bkernrbf_kernel(
+    tc, x, w1_words, w1_scales, w2_words, w2_scales, sh, d0, wo_words, wo_scales, dy, old, out
+):
+    nc = tc.nc
+    with ExitStack() as ctx:
+        sb = ctx.enter_context(tc.tile_pool(name="sb", bufs=1))
+        ps = ctx.enter_context(tc.psum_pool(name="ps", bufs=1))
+        ctx.enter_context(tc.manual_schedule())
+
+        def rows(t):
+            g, h = TILES[t]
+            return g, slice(h * P, (h + 1) * P)
+
+        planes = {}
+        words = {}
+        for name in ("w1", "w2", "wo"):
+            planes[name] = sb.tile([P, M], U8, name="plane_" + name, align_bytes=64)
+            words[name] = sb.tile([P, 2 * M], U8, name="words_" + name, align_bytes=64)
+            nc.vector.memset(planes[name][:].bitcast(I32), 0)
+        sh_rows = sb.tile([P, P], F32, name="sh_rows", align_bytes=64)
+        nc.vector.memset(sh_rows[:], 0.0)
+
+        def load_words(queue, name, src):
+            queue.dma_start(out=words[name][:].bitcast(I32), in_=src.rearrange("g p b -> (g p) b").bitcast(I32))
+
+        def load_scales(queue, name, src):
+            flat = src.rearrange("g f m -> (g f) m").bitcast(I32)
+            for q in range(P // QUAD):
+                queue.dma_start(
+                    out=planes[name][QUAD * q : QUAD * q + 4, :].bitcast(I32), in_=flat[4 * q : 4 * q + 4, :]
+                )
+
+        x_raw = sb.tile([P, PACK, N], F32, name="x_raw")
+        nc.sync.dma_start(out=x_raw[:], in_=x.rearrange("g (p j) n -> (g p) j n", j=PACK))
+        load_scales(nc.sync, "w1", w1_scales)
+        load_words(nc.sync, "w1", w1_words)
+        dy_rows = dy.rearrange("g (p j) n -> (g p) j n", j=PACK)
+        dy_raw = []
+        for u in range(2):
+            part = sb.tile([P, PACK, HALF], F32, name="dy_raw%d" % u)
+            nc.sync.dma_start(out=part[:], in_=dy_rows[:, :, u * HALF : (u + 1) * HALF])
+            dy_raw.append(part)
+        load_words(nc.sync, "w2", w2_words)
+        load_words(nc.sync, "wo", wo_words)
+        load_scales(nc.sync, "wo", wo_scales)
+        nc.gpsimd.dma_start(
+            out=sh_rows[0:P:QUAD, :].rearrange("q (c j) -> q c j", j=QUAD),
+            in_=sh.rearrange("g (h q j) o -> q (g h) (j o)", h=M // P, j=QUAD),
+        )
+        load_scales(nc.gpsimd, "w2", w2_scales)
+        d0_sb, old_sb = [], []
+        for src, tiles, name in ((d0, d0_sb, "d0"), (old, old_sb, "old")):
+            for t in range(len(TILES)):
+                g, r = rows(t)
+                part = sb.tile([P, N], F32, name="%s_%d" % (name, t))
+                nc.sync.dma_start(out=part[:], in_=src[g, r, :])
+                tiles.append(part)
+
+        x_packed = sb.tile([P, N, PACK], BF16, name="x_packed", align_bytes=64)
+        x_codes = sb.tile([P, N], U32, name="x_codes", align_bytes=64)
+        x_scales = sb.tile([P, N], U8, name="x_scales", align_bytes=64)
+        interleave(nc.vector.tensor_copy, x_packed, x_raw, 0, X_VECTOR_COLS)
+        interleave(nc.scalar.copy, x_packed, x_raw, X_VECTOR_COLS, N)
+        nc.vector.quantize_mx(
+            out=x_codes[:].bitcast(FP8X4), scales=x_scales[:], in_=x_packed[:].rearrange("p n j -> p (n j)")
+        )
+
+        sh_t = sb.tile([P, P], F32, name="sh_t", align_bytes=64)
+        nc.vector.transpose(out=sh_t[:], in_=sh_rows[:])
+        sh2 = sb.tile([P, P // QUAD], F32, name="sh2")
+        nc.vector.tensor_scalar(out=sh2[:], in0=sh_t[:, 0:P:QUAD], scalar1=2.0, scalar2=None, op0=ALU.mult)
+
+        bank_a, bank_b = [], []
+        for t in range(len(TILES)):
+            bank_a.append(ps.tile([P, N], F32, name="bank_a%d" % t))
+            bank_b.append(ps.tile([P, N], F32, name="bank_b%d" % t))
+
+        def product(bank, name, codes, scales, t):
+            g, h = TILES[t]
+            tile_rows = slice(ROWS * g, ROWS * (g + 1))
+            nc.tensor.matmul_mx(
+                out=bank[:],
+                lhsT=words[name][tile_rows, 2 * P * h : 2 * P * (h + 1)].bitcast(FP4X4),
+                lhsT_scale=planes[name][tile_rows, P * h : P * (h + 1)],
+                rhs=codes[tile_rows, :].bitcast(FP8X4),
+                rhs_scale=scales[tile_rows, :],
+                start=True,
+                stop=True,
+            )
+
+        for t in range(len(TILES)):
+            product(bank_a[t], "w1", x_codes, x_scales, t)
+        for t in range(len(TILES)):
+            product(bank_b[t], "w2", x_codes, x_scales, t)
+
+        dy_codes = sb.tile([P, N], U32, name="dy_codes", align_bytes=64)
+        dy_scales = sb.tile([P, N], U8, name="dy_scales", align_bytes=64)
+        dy_packed = []
+        for u in range(2):
+            part = sb.tile([P, HALF, PACK], BF16, name="dy_packed%d" % u, align_bytes=64)
+            dy_packed.append(part)
+
+        def quantize_dy(u):
+            cols = slice(u * HALF, (u + 1) * HALF)
+            nc.vector.quantize_mx(
+                out=dy_codes[:, cols].bitcast(FP8X4),
+                scales=dy_scales[:, cols],
+                in_=dy_packed[u][:].rearrange("p n j -> p (n j)"),
+            )
+
+        interleave(nc.vector.tensor_copy, dy_packed[0], dy_raw[0], 0, DY_VECTOR_COLS)
+        interleave(nc.scalar.copy, dy_packed[0], dy_raw[0], DY_VECTOR_COLS, HALF)
+        quantize_dy(0)
+        interleave(nc.vector.tensor_copy, dy_packed[1], dy_raw[1], 0, DY_VECTOR_COLS)
+        interleave(nc.scalar.copy, dy_packed[1], dy_raw[1], DY_VECTOR_COLS, HALF)
+        quantize_dy(1)
+
+        work, weight = [], []
+        for t in range(len(TILES)):
+            work.append(sb.tile([P, N], F32, name="work%d" % t))
+            weight.append(sb.tile([P, N], F32, name="weight%d" % t))
+
+        def column(t):
+            g, h = TILES[t]
+            return (M // P) * g + h
+
+        def distance(t):
+            c = column(t)
+            nc.vector.scalar_tensor_tensor(
+                out=work[t][:], in0=bank_a[t][:], scalar=2.0, in1=d0_sb[t][:], op0=ALU.mult, op1=ALU.subtract
+            )
+            nc.scalar.activation(
+                out=weight[t][:], in_=work[t][:], func=ACT.Exp, scale=sh_t[:, QUAD * c : QUAD * c + 1]
+            )
+            product(bank_a[t], "wo", dy_codes, dy_scales, t)
+
+        def weigh(t):
+            nc.vector.tensor_tensor(out=work[t][:], in0=bank_b[t][:], in1=weight[t][:], op=ALU.mult)
+
+        def chain(t):
+            c = column(t)
+            nc.vector.scalar_tensor_tensor(
+                out=weight[t][:], in0=bank_a[t][:], scalar=sh2[:, c : c + 1], in1=work[t][:],
+                op0=ALU.mult, op1=ALU.mult,
+            )
+
+        def finish(engine, t):
+            g, r = rows(t)
+            engine.tensor_tensor(out=work[t][:], in0=weight[t][:], in1=old_sb[t][:], op=ALU.add)
+            nc.sync.dma_start(out=out[g, r, :], in_=work[t][:])
+
+        distance(0)
+        distance(1)
+        weigh(0)
+        distance(2)
+        chain(0)
+        finish(nc.gpsimd, 0)
+        weigh(1)
+        distance(3)
+        chain(1)
+        finish(nc.gpsimd, 1)
+        weigh(2)
+        weigh(3)
+        chain(2)
+        chain(3)
+        finish(nc.vector, 2)
+        finish(nc.vector, 3)

@@ -66,29 +66,31 @@ def tile_rows_bkernrbf_kernel(
 
         x_raw = sb.tile([P, PACK, N], F32, name="x_raw")
         nc.sync.dma_start(out=x_raw[:], in_=x.rearrange("g (p j) n -> (g p) j n", j=PACK))
-        load_scales(nc.sync, "w1", w1_scales)
         load_words(nc.sync, "w1", w1_words)
+        load_scales(nc.sync, "w1", w1_scales)
         dy_rows = dy.rearrange("g (p j) n -> (g p) j n", j=PACK)
         dy_raw = []
         for u in range(2):
             part = sb.tile([P, PACK, HALF], F32, name="dy_raw%d" % u)
             nc.sync.dma_start(out=part[:], in_=dy_rows[:, :, u * HALF : (u + 1) * HALF])
             dy_raw.append(part)
+
+        def load_pair(src, name, h):
+            pair = sb.tile([P, G, N], F32, name="%s_%d" % (name, h))
+            nc.sync.dma_start(out=pair[:], in_=src[:, h * P : (h + 1) * P, :].rearrange("g p n -> p g n"))
+            return [pair[:, g, :] for g in range(G)]
+
+        d0_sb = load_pair(d0, "d0", 0)
         load_words(nc.sync, "w2", w2_words)
-        load_words(nc.sync, "wo", wo_words)
-        load_scales(nc.sync, "wo", wo_scales)
+        load_scales(nc.sync, "w2", w2_scales)
+        d0_sb = d0_sb + load_pair(d0, "d0", 1)
+        old_sb = load_pair(old, "old", 0) + load_pair(old, "old", 1)
+        load_words(nc.gpsimd, "wo", wo_words)
         nc.gpsimd.dma_start(
             out=sh_rows[0:P:QUAD, :].rearrange("q (c j) -> q c j", j=QUAD),
             in_=sh.rearrange("g (h q j) o -> q (g h) (j o)", h=M // P, j=QUAD),
         )
-        load_scales(nc.gpsimd, "w2", w2_scales)
-        d0_sb, old_sb = [], []
-        for src, tiles, name in ((d0, d0_sb, "d0"), (old, old_sb, "old")):
-            for t in range(len(TILES)):
-                g, r = rows(t)
-                part = sb.tile([P, N], F32, name="%s_%d" % (name, t))
-                nc.sync.dma_start(out=part[:], in_=src[g, r, :])
-                tiles.append(part)
+        load_scales(nc.gpsimd, "wo", wo_scales)
 
         x_packed = sb.tile([P, N, PACK], BF16, name="x_packed", align_bytes=64)
         x_codes = sb.tile([P, N], U32, name="x_codes", align_bytes=64)
@@ -142,8 +144,7 @@ def tile_rows_bkernrbf_kernel(
                 in_=dy_packed[u][:].rearrange("p n j -> p (n j)"),
             )
 
-        interleave(nc.vector.tensor_copy, dy_packed[0], dy_raw[0], 0, DY_VECTOR_COLS)
-        interleave(nc.scalar.copy, dy_packed[0], dy_raw[0], DY_VECTOR_COLS, HALF)
+        interleave(nc.scalar.copy, dy_packed[0], dy_raw[0], 0, HALF)
         quantize_dy(0)
         interleave(nc.vector.tensor_copy, dy_packed[1], dy_raw[1], 0, DY_VECTOR_COLS)
         interleave(nc.scalar.copy, dy_packed[1], dy_raw[1], DY_VECTOR_COLS, HALF)
@@ -161,41 +162,47 @@ def tile_rows_bkernrbf_kernel(
         def distance(t):
             c = column(t)
             nc.vector.scalar_tensor_tensor(
-                out=work[t][:], in0=bank_a[t][:], scalar=2.0, in1=d0_sb[t][:], op0=ALU.mult, op1=ALU.subtract
+                out=work[t][:], in0=bank_a[t][:], scalar=2.0, in1=d0_sb[t], op0=ALU.mult, op1=ALU.subtract
             )
             nc.scalar.activation(
                 out=weight[t][:], in_=work[t][:], func=ACT.Exp, scale=sh_t[:, QUAD * c : QUAD * c + 1]
             )
             product(bank_a[t], "wo", dy_codes, dy_scales, t)
 
-        def weigh(t):
-            nc.vector.tensor_tensor(out=work[t][:], in0=bank_b[t][:], in1=weight[t][:], op=ALU.mult)
+        def weigh(t, cols=slice(0, N)):
+            nc.vector.tensor_tensor(out=work[t][:, cols], in0=bank_b[t][:, cols], in1=weight[t][:, cols], op=ALU.mult)
 
-        def chain(t):
+        def chain(t, cols=slice(0, N)):
             c = column(t)
             nc.vector.scalar_tensor_tensor(
-                out=weight[t][:], in0=bank_a[t][:], scalar=sh2[:, c : c + 1], in1=work[t][:],
+                out=weight[t][:, cols], in0=bank_a[t][:, cols], scalar=sh2[:, c : c + 1], in1=work[t][:, cols],
                 op0=ALU.mult, op1=ALU.mult,
             )
 
-        def finish(engine, t):
+        def finish(engine, t, cols=slice(0, N)):
             g, r = rows(t)
-            engine.tensor_tensor(out=work[t][:], in0=weight[t][:], in1=old_sb[t][:], op=ALU.add)
-            nc.sync.dma_start(out=out[g, r, :], in_=work[t][:])
+            engine.tensor_tensor(out=work[t][:, cols], in0=weight[t][:, cols], in1=old_sb[t][:, cols], op=ALU.add)
+            nc.sync.dma_start(out=out[g, r, cols], in_=work[t][:, cols])
 
+        z2_first = sb.tile([P, N], F32, name="z2_first")
+        nc.scalar.copy(out=z2_first[:], in_=bank_b[0][:])
         distance(0)
+        nc.gpsimd.tensor_tensor(out=work[0][:], in0=z2_first[:], in1=weight[0][:], op=ALU.mult)
         distance(1)
-        weigh(0)
         distance(2)
+        weigh(1)
+        weigh(2)
         chain(0)
         finish(nc.gpsimd, 0)
-        weigh(1)
-        distance(3)
         chain(1)
         finish(nc.gpsimd, 1)
-        weigh(2)
-        weigh(3)
+        distance(3)
         chain(2)
-        chain(3)
+        halves = [slice(0, HALF), slice(HALF, N)]
+        for cols in halves:
+            weigh(3, cols)
+        for cols in halves:
+            chain(3, cols)
         finish(nc.vector, 2)
-        finish(nc.vector, 3)
+        for cols in halves:
+            finish(nc.vector, 3, cols)

@@ -22,7 +22,8 @@ QUAD = 32
 HALF = N // 2
 TILES = [(g, h) for h in range(M // P) for g in range(G)]
 X_VECTOR_COLS = 352
-DY_VECTOR_COLS = 176
+DY_FIRST_VECTOR_COLS = 112
+DY_VECTOR_COLS = 160
 
 
 def interleave(copy, packed, raw, c0, c1):
@@ -57,9 +58,9 @@ def tile_rows_bkernrbf_kernel(
         def load_words(queue, name, src):
             queue.dma_start(out=words[name][:].bitcast(I32), in_=src.rearrange("g p b -> (g p) b").bitcast(I32))
 
-        def load_scales(queue, name, src):
+        def load_scales(queue, name, src, quadrants=range(P // QUAD)):
             flat = src.rearrange("g f m -> (g f) m").bitcast(I32)
-            for q in range(P // QUAD):
+            for q in quadrants:
                 queue.dma_start(
                     out=planes[name][QUAD * q : QUAD * q + 4, :].bitcast(I32), in_=flat[4 * q : 4 * q + 4, :]
                 )
@@ -80,17 +81,19 @@ def tile_rows_bkernrbf_kernel(
             nc.sync.dma_start(out=pair[:], in_=src[:, h * P : (h + 1) * P, :].rearrange("g p n -> p g n"))
             return [pair[:, g, :] for g in range(G)]
 
-        d0_sb = load_pair(d0, "d0", 0)
-        load_words(nc.sync, "w2", w2_words)
-        load_scales(nc.sync, "w2", w2_scales)
-        d0_sb = d0_sb + load_pair(d0, "d0", 1)
-        old_sb = load_pair(old, "old", 0) + load_pair(old, "old", 1)
-        load_words(nc.gpsimd, "wo", wo_words)
-        nc.gpsimd.dma_start(
+        nc.sync.dma_start(
             out=sh_rows[0:P:QUAD, :].rearrange("q (c j) -> q c j", j=QUAD),
             in_=sh.rearrange("g (h q j) o -> q (g h) (j o)", h=M // P, j=QUAD),
         )
-        load_scales(nc.gpsimd, "wo", wo_scales)
+        load_words(nc.sync, "w2", w2_words)
+        load_scales(nc.sync, "w2", w2_scales, range(2))
+        d0_sb = load_pair(d0, "d0", 0)
+        load_scales(nc.sync, "w2", w2_scales, range(2, 3))
+        d0_sb = d0_sb + load_pair(d0, "d0", 1)
+        load_scales(nc.sync, "w2", w2_scales, range(3, 4))
+        load_words(nc.sync, "wo", wo_words)
+        load_scales(nc.sync, "wo", wo_scales)
+        old_sb = load_pair(old, "old", 0) + load_pair(old, "old", 1)
 
         x_packed = sb.tile([P, N, PACK], BF16, name="x_packed", align_bytes=64)
         x_codes = sb.tile([P, N], U32, name="x_codes", align_bytes=64)
@@ -100,11 +103,6 @@ def tile_rows_bkernrbf_kernel(
         nc.vector.quantize_mx(
             out=x_codes[:].bitcast(FP8X4), scales=x_scales[:], in_=x_packed[:].rearrange("p n j -> p (n j)")
         )
-
-        sh_t = sb.tile([P, P], F32, name="sh_t", align_bytes=64)
-        nc.vector.transpose(out=sh_t[:], in_=sh_rows[:])
-        sh2 = sb.tile([P, P // QUAD], F32, name="sh2")
-        nc.vector.tensor_scalar(out=sh2[:], in0=sh_t[:, 0:P:QUAD], scalar1=2.0, scalar2=None, op0=ALU.mult)
 
         bank_a, bank_b = [], []
         for t in range(len(TILES)):
@@ -124,10 +122,12 @@ def tile_rows_bkernrbf_kernel(
                 stop=True,
             )
 
-        for t in range(len(TILES)):
-            product(bank_a[t], "w1", x_codes, x_scales, t)
-        for t in range(len(TILES)):
-            product(bank_b[t], "w2", x_codes, x_scales, t)
+        product(bank_a[0], "w1", x_codes, x_scales, 0)
+        product(bank_a[1], "w1", x_codes, x_scales, 1)
+        product(bank_b[0], "w2", x_codes, x_scales, 0)
+        product(bank_a[2], "w1", x_codes, x_scales, 2)
+        product(bank_a[3], "w1", x_codes, x_scales, 3)
+        product(bank_b[1], "w2", x_codes, x_scales, 1)
 
         dy_codes = sb.tile([P, N], U32, name="dy_codes", align_bytes=64)
         dy_scales = sb.tile([P, N], U8, name="dy_scales", align_bytes=64)
@@ -144,11 +144,17 @@ def tile_rows_bkernrbf_kernel(
                 in_=dy_packed[u][:].rearrange("p n j -> p (n j)"),
             )
 
-        interleave(nc.scalar.copy, dy_packed[0], dy_raw[0], 0, HALF)
+        interleave(nc.vector.tensor_copy, dy_packed[0], dy_raw[0], 0, DY_FIRST_VECTOR_COLS)
+        interleave(nc.scalar.copy, dy_packed[0], dy_raw[0], DY_FIRST_VECTOR_COLS, HALF)
         quantize_dy(0)
         interleave(nc.vector.tensor_copy, dy_packed[1], dy_raw[1], 0, DY_VECTOR_COLS)
         interleave(nc.scalar.copy, dy_packed[1], dy_raw[1], DY_VECTOR_COLS, HALF)
+        sh_t = sb.tile([P, P], F32, name="sh_t", align_bytes=64)
+        nc.vector.transpose(out=sh_t[:], in_=sh_rows[:])
         quantize_dy(1)
+
+        sh2 = sb.tile([P, P // QUAD], F32, name="sh2")
+        nc.vector.tensor_scalar(out=sh2[:], in0=sh_t[:, 0:P:QUAD], scalar1=2.0, scalar2=None, op0=ALU.mult)
 
         work, weight = [], []
         for t in range(len(TILES)):
@@ -189,20 +195,19 @@ def tile_rows_bkernrbf_kernel(
         distance(0)
         nc.gpsimd.tensor_tensor(out=work[0][:], in0=z2_first[:], in1=weight[0][:], op=ALU.mult)
         distance(1)
+        product(bank_b[2], "w2", x_codes, x_scales, 2)
+        product(bank_b[3], "w2", x_codes, x_scales, 3)
         distance(2)
+        distance(3)
         weigh(1)
-        weigh(2)
         chain(0)
         finish(nc.gpsimd, 0)
         chain(1)
         finish(nc.gpsimd, 1)
-        distance(3)
+        weigh(2)
+        weigh(3)
         chain(2)
-        halves = [slice(0, HALF), slice(HALF, N)]
-        for cols in halves:
-            weigh(3, cols)
-        for cols in halves:
-            chain(3, cols)
+        chain(3)
         finish(nc.vector, 2)
-        for cols in halves:
+        for cols in (slice(0, HALF), slice(HALF, N)):
             finish(nc.vector, 3, cols)

@@ -20,10 +20,9 @@ PACK = 4
 ROWS = D // PACK
 QUAD = 32
 HALF = N // 2
-TILES = [(g, h) for h in range(M // P) for g in range(G)]
-X_VECTOR_COLS = 352
-DY_FIRST_VECTOR_COLS = 112
-DY_VECTOR_COLS = 160
+TILES = [(g, h) for g in range(G) for h in range(M // P)]
+X_VECTOR_COLS = (176, 128)
+DY_VECTOR_COLS = (160, 160)
 
 
 def interleave(copy, packed, raw, c0, c1):
@@ -51,8 +50,9 @@ def tile_rows_bkernrbf_kernel(
         for name in ("w1", "w2", "wo"):
             planes[name] = sb.tile([P, M], U8, name="plane_" + name, align_bytes=64)
             words[name] = sb.tile([P, 2 * M], U8, name="words_" + name, align_bytes=64)
-            nc.vector.memset(planes[name][:].bitcast(I32), 0)
         sh_rows = sb.tile([P, P], F32, name="sh_rows", align_bytes=64)
+        for name in ("w1", "w2", "wo"):
+            nc.vector.memset(planes[name][:].bitcast(I32), 0)
         nc.vector.memset(sh_rows[:], 0.0)
 
         def load_words(queue, name, src):
@@ -68,7 +68,9 @@ def tile_rows_bkernrbf_kernel(
         x_raw = sb.tile([P, PACK, N], F32, name="x_raw")
         nc.sync.dma_start(out=x_raw[:], in_=x.rearrange("g (p j) n -> (g p) j n", j=PACK))
         load_words(nc.sync, "w1", w1_words)
-        load_scales(nc.sync, "w1", w1_scales)
+        load_words(nc.sync, "w2", w2_words)
+        load_scales(nc.sync, "w1", w1_scales, range(2))
+        load_scales(nc.sync, "w2", w2_scales, range(1))
         dy_rows = dy.rearrange("g (p j) n -> (g p) j n", j=PACK)
         dy_raw = []
         for u in range(2):
@@ -76,33 +78,49 @@ def tile_rows_bkernrbf_kernel(
             nc.sync.dma_start(out=part[:], in_=dy_rows[:, :, u * HALF : (u + 1) * HALF])
             dy_raw.append(part)
 
-        def load_pair(src, name, h):
-            pair = sb.tile([P, G, N], F32, name="%s_%d" % (name, h))
-            nc.sync.dma_start(out=pair[:], in_=src[:, h * P : (h + 1) * P, :].rearrange("g p n -> p g n"))
-            return [pair[:, g, :] for g in range(G)]
+        def load_pair(src, name, g):
+            pair = sb.tile([P, M // P, N], F32, name="%s_%d" % (name, g))
+            nc.sync.dma_start(out=pair[:], in_=src[g].rearrange("(h p) n -> p h n", p=P))
+            return [pair[:, h, :] for h in range(M // P)]
 
+        def load_tile(src, name, t):
+            g, r = rows(t)
+            part = sb.tile([P, N], F32, name="%s_tile%d" % (name, t))
+            nc.sync.dma_start(out=part[:], in_=src[g, r, :])
+            return [part[:]]
+
+        load_scales(nc.sync, "w2", w2_scales, range(1, 2))
         nc.sync.dma_start(
             out=sh_rows[0:P:QUAD, :].rearrange("q (c j) -> q c j", j=QUAD),
             in_=sh.rearrange("g (h q j) o -> q (g h) (j o)", h=M // P, j=QUAD),
         )
-        load_words(nc.sync, "w2", w2_words)
-        load_scales(nc.sync, "w2", w2_scales, range(2))
-        d0_sb = load_pair(d0, "d0", 0)
-        load_scales(nc.sync, "w2", w2_scales, range(2, 3))
-        d0_sb = d0_sb + load_pair(d0, "d0", 1)
-        load_scales(nc.sync, "w2", w2_scales, range(3, 4))
+        d0_sb = load_tile(d0, "d0", 0)
+        load_scales(nc.sync, "w1", w1_scales, range(2, 4))
+        d0_sb = d0_sb + load_tile(d0, "d0", 1) + load_pair(d0, "d0", 1)
+        load_scales(nc.sync, "wo", wo_scales, range(2))
         load_words(nc.sync, "wo", wo_words)
-        load_scales(nc.sync, "wo", wo_scales)
-        old_sb = load_pair(old, "old", 0) + load_pair(old, "old", 1)
+        load_scales(nc.sync, "w2", w2_scales, range(2, 4))
+        old_sb = load_pair(old, "old", 0)
+        load_scales(nc.sync, "wo", wo_scales, range(2, 4))
+        old_sb = old_sb + load_pair(old, "old", 1)
 
-        x_packed = sb.tile([P, N, PACK], BF16, name="x_packed", align_bytes=64)
+        def quantize(codes, scales, packed, u):
+            cols = slice(u * HALF, (u + 1) * HALF)
+            nc.vector.quantize_mx(
+                out=codes[:, cols].bitcast(FP8X4), scales=scales[:, cols], in_=packed[:].rearrange("p n j -> p (n j)")
+            )
+
         x_codes = sb.tile([P, N], U32, name="x_codes", align_bytes=64)
         x_scales = sb.tile([P, N], U8, name="x_scales", align_bytes=64)
-        interleave(nc.vector.tensor_copy, x_packed, x_raw, 0, X_VECTOR_COLS)
-        interleave(nc.scalar.copy, x_packed, x_raw, X_VECTOR_COLS, N)
-        nc.vector.quantize_mx(
-            out=x_codes[:].bitcast(FP8X4), scales=x_scales[:], in_=x_packed[:].rearrange("p n j -> p (n j)")
-        )
+        x_packed = []
+        for u in range(2):
+            part = sb.tile([P, HALF, PACK], BF16, name="x_packed%d" % u, align_bytes=64)
+            raw = x_raw[:, :, u * HALF : (u + 1) * HALF]
+            interleave(nc.vector.tensor_copy, part, raw, 0, X_VECTOR_COLS[u])
+            interleave(nc.scalar.copy, part, raw, X_VECTOR_COLS[u], HALF)
+            x_packed.append(part)
+        for u in range(2):
+            quantize(x_codes, x_scales, x_packed[u], u)
 
         bank_a, bank_b = [], []
         for t in range(len(TILES)):
@@ -123,38 +141,25 @@ def tile_rows_bkernrbf_kernel(
             )
 
         product(bank_a[0], "w1", x_codes, x_scales, 0)
+        product(bank_b[1], "w2", x_codes, x_scales, 1)
         product(bank_a[1], "w1", x_codes, x_scales, 1)
         product(bank_b[0], "w2", x_codes, x_scales, 0)
         product(bank_a[2], "w1", x_codes, x_scales, 2)
         product(bank_a[3], "w1", x_codes, x_scales, 3)
-        product(bank_b[1], "w2", x_codes, x_scales, 1)
 
         dy_codes = sb.tile([P, N], U32, name="dy_codes", align_bytes=64)
         dy_scales = sb.tile([P, N], U8, name="dy_scales", align_bytes=64)
         dy_packed = []
         for u in range(2):
             part = sb.tile([P, HALF, PACK], BF16, name="dy_packed%d" % u, align_bytes=64)
+            interleave(nc.vector.tensor_copy, part, dy_raw[u], 0, DY_VECTOR_COLS[u])
+            interleave(nc.scalar.copy, part, dy_raw[u], DY_VECTOR_COLS[u], HALF)
             dy_packed.append(part)
+            if u == 0:
+                quantize(dy_codes, dy_scales, part, u)
 
-        def quantize_dy(u):
-            cols = slice(u * HALF, (u + 1) * HALF)
-            nc.vector.quantize_mx(
-                out=dy_codes[:, cols].bitcast(FP8X4),
-                scales=dy_scales[:, cols],
-                in_=dy_packed[u][:].rearrange("p n j -> p (n j)"),
-            )
-
-        interleave(nc.vector.tensor_copy, dy_packed[0], dy_raw[0], 0, DY_FIRST_VECTOR_COLS)
-        interleave(nc.scalar.copy, dy_packed[0], dy_raw[0], DY_FIRST_VECTOR_COLS, HALF)
-        quantize_dy(0)
-        interleave(nc.vector.tensor_copy, dy_packed[1], dy_raw[1], 0, DY_VECTOR_COLS)
-        interleave(nc.scalar.copy, dy_packed[1], dy_raw[1], DY_VECTOR_COLS, HALF)
         sh_t = sb.tile([P, P], F32, name="sh_t", align_bytes=64)
         nc.vector.transpose(out=sh_t[:], in_=sh_rows[:])
-        quantize_dy(1)
-
-        sh2 = sb.tile([P, P // QUAD], F32, name="sh2")
-        nc.vector.tensor_scalar(out=sh2[:], in0=sh_t[:, 0:P:QUAD], scalar1=2.0, scalar2=None, op0=ALU.mult)
 
         work, weight = [], []
         for t in range(len(TILES)):
@@ -173,15 +178,20 @@ def tile_rows_bkernrbf_kernel(
             nc.scalar.activation(
                 out=weight[t][:], in_=work[t][:], func=ACT.Exp, scale=sh_t[:, QUAD * c : QUAD * c + 1]
             )
+
+        def gradient(t):
             product(bank_a[t], "wo", dy_codes, dy_scales, t)
 
         def weigh(t, cols=slice(0, N)):
-            nc.vector.tensor_tensor(out=work[t][:, cols], in0=bank_b[t][:, cols], in1=weight[t][:, cols], op=ALU.mult)
+            nc.vector.scalar_tensor_tensor(
+                out=work[t][:, cols], in0=bank_b[t][:, cols], scalar=2.0, in1=weight[t][:, cols],
+                op0=ALU.mult, op1=ALU.mult,
+            )
 
         def chain(t, cols=slice(0, N)):
             c = column(t)
             nc.vector.scalar_tensor_tensor(
-                out=weight[t][:, cols], in0=bank_a[t][:, cols], scalar=sh2[:, c : c + 1], in1=work[t][:, cols],
+                out=weight[t][:, cols], in0=bank_a[t][:, cols], scalar=sh_t[:, QUAD * c : QUAD * c + 1], in1=work[t][:, cols],
                 op0=ALU.mult, op1=ALU.mult,
             )
 
@@ -190,21 +200,25 @@ def tile_rows_bkernrbf_kernel(
             engine.tensor_tensor(out=work[t][:, cols], in0=weight[t][:, cols], in1=old_sb[t][:, cols], op=ALU.add)
             nc.sync.dma_start(out=out[g, r, cols], in_=work[t][:, cols])
 
-        z2_first = sb.tile([P, N], F32, name="z2_first")
-        nc.scalar.copy(out=z2_first[:], in_=bank_b[0][:])
+        z2_second = sb.tile([P, N], F32, name="z2_second")
+        nc.scalar.activation(out=z2_second[:], in_=bank_b[1][:], func=ACT.Copy, scale=2.0)
         distance(0)
-        nc.gpsimd.tensor_tensor(out=work[0][:], in0=z2_first[:], in1=weight[0][:], op=ALU.mult)
-        distance(1)
+        quantize(dy_codes, dy_scales, dy_packed[1], 1)
+        gradient(0)
         product(bank_b[2], "w2", x_codes, x_scales, 2)
+        distance(1)
+        gradient(1)
         product(bank_b[3], "w2", x_codes, x_scales, 3)
-        distance(2)
-        distance(3)
-        weigh(1)
+        nc.gpsimd.tensor_tensor(out=work[1][:], in0=z2_second[:], in1=weight[1][:], op=ALU.mult)
+        weigh(0)
+        for t in (2, 3):
+            distance(t)
+            gradient(t)
         chain(0)
         finish(nc.gpsimd, 0)
+        weigh(2)
         chain(1)
         finish(nc.gpsimd, 1)
-        weigh(2)
         weigh(3)
         chain(2)
         chain(3)

from contextlib import ExitStack

import concourse.mybir as mybir

G, D, M, N = 2, 256, 256, 512
FLOPS = 3 * 2 * G * D * M * N

F32 = mybir.dt.float32
BF16 = mybir.dt.bfloat16
I32 = mybir.dt.int32
U32 = mybir.dt.uint32
U8 = mybir.dt.uint8
FP8X4 = mybir.dt.float8_e4m3fn_x4
FP4X4 = mybir.dt.float4_e2m1fn_x4
ALU = mybir.AluOpType
ACT = mybir.ActivationFunctionType

P = 128
PACK = 4
ROWS = D // PACK
QUAD = 32
HALF = N // 2
TILES = [(g, h) for g in range(G) for h in range(M // P)]
X_VECTOR_COLS = (176, 128)
DY_VECTOR_COLS = (160, 160)


def interleave(copy, packed, raw, c0, c1):
    copy(
        out=packed[:, c0:c1, :].rearrange("p (c i) j -> p c j i", i=4),
        in_=raw[:, :, c0:c1].rearrange("p j (c i) -> p c j i", i=4),
    )


def tile_rows_bkernrbf_kernel(
    tc, x, w1_words, w1_scales, w2_words, w2_scales, sh, d0, wo_words, wo_scales, dy, old, out
):
    nc = tc.nc
    with ExitStack() as ctx:
        sb = ctx.enter_context(tc.tile_pool(name="sb", bufs=1))
        ps = ctx.enter_context(tc.psum_pool(name="ps", bufs=1))
        ctx.enter_context(tc.manual_schedule())

        def rows(t):
            g, h = TILES[t]
            return g, slice(h * P, (h + 1) * P)

        planes = {}
        words = {}
        for name in ("w1", "w2", "wo"):
            planes[name] = sb.tile([P, M], U8, name="plane_" + name, align_bytes=64)
            words[name] = sb.tile([P, 2 * M], U8, name="words_" + name, align_bytes=64)
        sh_rows = sb.tile([P, P], F32, name="sh_rows", align_bytes=64)
        for name in ("w1", "w2", "wo"):
            nc.vector.memset(planes[name][:].bitcast(I32), 0)
        nc.vector.memset(sh_rows[:], 0.0)

        def load_words(queue, name, src):
            queue.dma_start(out=words[name][:].bitcast(I32), in_=src.rearrange("g p b -> (g p) b").bitcast(I32))

        def load_scales(queue, name, src, quadrants=range(P // QUAD)):
            flat = src.rearrange("g f m -> (g f) m").bitcast(I32)
            for q in quadrants:
                queue.dma_start(
                    out=planes[name][QUAD * q : QUAD * q + 4, :].bitcast(I32), in_=flat[4 * q : 4 * q + 4, :]
                )

        x_raw = sb.tile([P, PACK, N], F32, name="x_raw")
        nc.sync.dma_start(out=x_raw[:], in_=x.rearrange("g (p j) n -> (g p) j n", j=PACK))
        load_words(nc.sync, "w1", w1_words)
        load_words(nc.sync, "w2", w2_words)
        load_scales(nc.sync, "w1", w1_scales, range(2))
        load_scales(nc.sync, "w2", w2_scales, range(1))
        dy_rows = dy.rearrange("g (p j) n -> (g p) j n", j=PACK)
        dy_raw = []
        for u in range(2):
            part = sb.tile([P, PACK, HALF], F32, name="dy_raw%d" % u)
            nc.sync.dma_start(out=part[:], in_=dy_rows[:, :, u * HALF : (u + 1) * HALF])
            dy_raw.append(part)

        def load_pair(src, name, g):
            pair = sb.tile([P, M // P, N], F32, name="%s_%d" % (name, g))
            nc.sync.dma_start(out=pair[:], in_=src[g].rearrange("(h p) n -> p h n", p=P))
            return [pair[:, h, :] for h in range(M // P)]

        def load_tile(src, name, t):
            g, r = rows(t)
            part = sb.tile([P, N], F32, name="%s_tile%d" % (name, t))
            nc.sync.dma_start(out=part[:], in_=src[g, r, :])
            return [part[:]]

        load_scales(nc.sync, "w2", w2_scales, range(1, 2))
        nc.sync.dma_start(
            out=sh_rows[0:P:QUAD, :].rearrange("q (c j) -> q c j", j=QUAD),
            in_=sh.rearrange("g (h q j) o -> q (g h) (j o)", h=M // P, j=QUAD),
        )
        d0_sb = load_tile(d0, "d0", 0)
        load_scales(nc.sync, "w1", w1_scales, range(2, 4))
        d0_sb = d0_sb + load_tile(d0, "d0", 1) + load_pair(d0, "d0", 1)
        load_scales(nc.sync, "wo", wo_scales, range(2))
        load_words(nc.sync, "wo", wo_words)
        load_scales(nc.sync, "w2", w2_scales, range(2, 4))
        old_sb = load_pair(old, "old", 0)
        load_scales(nc.sync, "wo", wo_scales, range(2, 4))
        old_sb = old_sb + load_pair(old, "old", 1)

        def quantize(codes, scales, packed, u):
            cols = slice(u * HALF, (u + 1) * HALF)
            nc.vector.quantize_mx(
                out=codes[:, cols].bitcast(FP8X4), scales=scales[:, cols], in_=packed[:].rearrange("p n j -> p (n j)")
            )

        x_codes = sb.tile([P, N], U32, name="x_codes", align_bytes=64)
        x_scales = sb.tile([P, N], U8, name="x_scales", align_bytes=64)
        x_packed = []
        for u in range(2):
            part = sb.tile([P, HALF, PACK], BF16, name="x_packed%d" % u, align_bytes=64)
            raw = x_raw[:, :, u * HALF : (u + 1) * HALF]
            interleave(nc.vector.tensor_copy, part, raw, 0, X_VECTOR_COLS[u])
            interleave(nc.scalar.copy, part, raw, X_VECTOR_COLS[u], HALF)
            x_packed.append(part)
        for u in range(2):
            quantize(x_codes, x_scales, x_packed[u], u)

        bank_a, bank_b = [], []
        for t in range(len(TILES)):
            bank_a.append(ps.tile([P, N], F32, name="bank_a%d" % t))
            bank_b.append(ps.tile([P, N], F32, name="bank_b%d" % t))

        def product(bank, name, codes, scales, t):
            g, h = TILES[t]
            tile_rows = slice(ROWS * g, ROWS * (g + 1))
            nc.tensor.matmul_mx(
                out=bank[:],
                lhsT=words[name][tile_rows, 2 * P * h : 2 * P * (h + 1)].bitcast(FP4X4),
                lhsT_scale=planes[name][tile_rows, P * h : P * (h + 1)],
                rhs=codes[tile_rows, :].bitcast(FP8X4),
                rhs_scale=scales[tile_rows, :],
                start=True,
                stop=True,
            )

        product(bank_a[0], "w1", x_codes, x_scales, 0)
        product(bank_b[1], "w2", x_codes, x_scales, 1)
        product(bank_a[1], "w1", x_codes, x_scales, 1)
        product(bank_b[0], "w2", x_codes, x_scales, 0)
        product(bank_a[2], "w1", x_codes, x_scales, 2)
        product(bank_a[3], "w1", x_codes, x_scales, 3)

        dy_codes = sb.tile([P, N], U32, name="dy_codes", align_bytes=64)
        dy_scales = sb.tile([P, N], U8, name="dy_scales", align_bytes=64)
        dy_packed = []
        for u in range(2):
            part = sb.tile([P, HALF, PACK], BF16, name="dy_packed%d" % u, align_bytes=64)
            interleave(nc.vector.tensor_copy, part, dy_raw[u], 0, DY_VECTOR_COLS[u])
            interleave(nc.scalar.copy, part, dy_raw[u], DY_VECTOR_COLS[u], HALF)
            dy_packed.append(part)
            if u == 0:
                quantize(dy_codes, dy_scales, part, u)

        sh_t = sb.tile([P, P], F32, name="sh_t", align_bytes=64)
        nc.vector.transpose(out=sh_t[:], in_=sh_rows[:])

        work, weight = [], []
        for t in range(len(TILES)):
            work.append(sb.tile([P, N], F32, name="work%d" % t))
            weight.append(sb.tile([P, N], F32, name="weight%d" % t))

        def column(t):
            g, h = TILES[t]
            return (M // P) * g + h

        def distance(t):
            c = column(t)
            nc.vector.scalar_tensor_tensor(
                out=work[t][:], in0=bank_a[t][:], scalar=2.0, in1=d0_sb[t], op0=ALU.mult, op1=ALU.subtract
            )
            nc.scalar.activation(
                out=weight[t][:], in_=work[t][:], func=ACT.Exp, scale=sh_t[:, QUAD * c : QUAD * c + 1]
            )

        def gradient(t):
            product(bank_a[t], "wo", dy_codes, dy_scales, t)

        def weigh(t, cols=slice(0, N)):
            nc.vector.scalar_tensor_tensor(
                out=work[t][:, cols], in0=bank_b[t][:, cols], scalar=2.0, in1=weight[t][:, cols],
                op0=ALU.mult, op1=ALU.mult,
            )

        def chain(t, cols=slice(0, N)):
            c = column(t)
            nc.vector.scalar_tensor_tensor(
                out=weight[t][:, cols], in0=bank_a[t][:, cols], scalar=sh_t[:, QUAD * c : QUAD * c + 1], in1=work[t][:, cols],
                op0=ALU.mult, op1=ALU.mult,
            )

        def finish(engine, t, cols=slice(0, N)):
            g, r = rows(t)
            engine.tensor_tensor(out=work[t][:, cols], in0=weight[t][:, cols], in1=old_sb[t][:, cols], op=ALU.add)
            nc.sync.dma_start(out=out[g, r, cols], in_=work[t][:, cols])

        z2_second = sb.tile([P, N], F32, name="z2_second")
        nc.scalar.activation(out=z2_second[:], in_=bank_b[1][:], func=ACT.Copy, scale=2.0)
        distance(0)
        quantize(dy_codes, dy_scales, dy_packed[1], 1)
        gradient(0)
        product(bank_b[2], "w2", x_codes, x_scales, 2)
        distance(1)
        gradient(1)
        product(bank_b[3], "w2", x_codes, x_scales, 3)
        nc.gpsimd.tensor_tensor(out=work[1][:], in0=z2_second[:], in1=weight[1][:], op=ALU.mult)
        weigh(0)
        for t in (2, 3):
            distance(t)
            gradient(t)
        chain(0)
        finish(nc.gpsimd, 0)
        weigh(2)
        chain(1)
        finish(nc.gpsimd, 1)
        weigh(3)
        chain(2)
        chain(3)
        finish(nc.vector, 2)
        for cols in (slice(0, HALF), slice(HALF, N)):
            finish(nc.vector, 3, cols)
